import numpy as np
import ml_dtypes


def mxq(x, axis, fmt="e4m3"):
    dtype, down = {"e4m3": (ml_dtypes.float8_e4m3fn, 7), "e5m2": (ml_dtypes.float8_e5m2, 14)}[fmt]
    v = np.moveaxis(np.asarray(x, np.float32).astype(ml_dtypes.bfloat16).astype(np.float64), axis, -1)
    blocks = v.reshape(v.shape[:-1] + (-1, 32))
    amax = np.abs(blocks).max(-1, keepdims=True)
    byte = np.maximum(np.where(amax > 0, np.frexp(amax)[1] - 1 + 127, 0) - down, 1)
    scale = np.exp2(byte - 127.0)
    codes = (blocks / scale).astype(np.float32).astype(dtype).astype(np.float64)
    return np.moveaxis((codes * scale).reshape(v.shape), -1, axis)


WIDE = False


def mx_kscale(k):
    if not WIDE:
        return np.ones(k)
    levels = np.array([10, -10, 5, -5, 0])
    if k % 512:
        return np.exp2(np.random.permutation(np.resize(levels, k // 32))).repeat(32)
    a = np.empty((k // 512, 16))
    for p in range(k // 512):
        a[p, :8] = np.random.permutation(np.resize(levels, 8))
        for g in range(8):
            far = levels[np.abs(levels - a[p, g]) >= 10]
            a[p, g + 8] = far[np.random.randint(len(far))]
    return np.exp2(a.ravel()).repeat(32)


def f64(x):
    return np.asarray(x).astype(np.float64)


def striped(idx):
    return np.tile(idx.reshape(-1, 16).T, (8, 1)).astype(np.uint16)


def unstriped(offs):
    return offs[:16].T.reshape(-1).astype(np.int64)


E2M1 = np.array([0.0, 0.5, 1.0, 1.5, 2.0, 3.0, 4.0, 6.0, -0.0, -0.5, -1.0, -1.5, -2.0, -3.0, -4.0, -6.0])


def pack_fp4(w):
    k, n = w.shape
    w = f64(np.asarray(w, np.float32).astype(ml_dtypes.bfloat16)).reshape(k // 32, 32, n)
    amax = np.abs(w).max(1)
    mant, ex = np.frexp(amax / 6.0)
    byte = np.clip(np.where(amax > 0, np.where(mant > 0.5, ex, ex - 1) + 127, 1), 1, 254)
    scaled = (w * np.exp2(127.0 - byte)[:, None, :]).reshape(k, n).astype(np.float32)
    c = np.ascontiguousarray(scaled.reshape(k // 512, 128, 4, n).transpose(0, 1, 3, 2)).astype(ml_dtypes.float4_e2m1fn).view(np.uint8) & 0xF
    words = (c[..., 0::2] | (c[..., 1::2] << 4)).reshape(k // 512, 128, 2 * n)
    return np.ascontiguousarray(words), np.ascontiguousarray(byte.astype(np.uint8).reshape(k // 512, 16, n))


def unpack_fp4(words, scales):
    g, _, n = scales.shape
    words = np.ascontiguousarray(words).reshape(g, 128, n, 2)
    nib = np.empty((g, 128, n, 4), np.uint8)
    nib[..., 0::2] = words & 0xF
    nib[..., 1::2] = words >> 4
    vals = E2M1[nib] * np.repeat(np.exp2(scales.astype(np.float64) - 127.0), 8, axis=1)[..., None]
    return vals.transpose(0, 1, 3, 2).reshape(g * 512, n)


K, T, S, N, U = 512, 4096, 1024, 128, 2048


def setup_inputs():
    n = np.random.standard_normal
    s = mx_kscale(K)[:, None]
    packed_w1 = pack_fp4(n((K, N)) / np.sqrt(K) / s)
    return {
        "xT": (n((K, T)) * s).astype(np.float32),
        "mem": n((N, U)).astype(np.float32),
        "w1_words": packed_w1[0],
        "w1_scales": packed_w1[1],
        "offs": striped(np.random.permutation(T)[:S]),
        "slot": striped(np.random.permutation(U)[:S]),
    }


def reference(xT, mem, w1_words, w1_scales, offs, slot):
    xq = mxq(f64(xT)[:, unstriped(offs)], 0, "e4m3")
    y = unpack_fp4(w1_words, w1_scales).T @ xq
    out = f64(mem).copy()
    out[:, unstriped(slot)] = y
    return out

@@ -1,0 +1,107 @@
+from contextlib import ExitStack
+
+import concourse.mybir as mybir
+
+K, T, S, N, U = 512, 4096, 1024, 128, 2048
+FLOPS = 2 * K * N * S
+
+F32 = mybir.dt.float32
+BF16 = mybir.dt.bfloat16
+I32 = mybir.dt.int32
+U32 = mybir.dt.uint32
+U16 = mybir.dt.uint16
+U8 = mybir.dt.uint8
+FP8X4 = mybir.dt.float8_e4m3fn_x4
+FP4X4 = mybir.dt.float4_e2m1fn_x4
+COPY = mybir.ActivationFunctionType.Copy
+
+P = 128
+PACK = 4
+HALF = S // 2
+EARLY_ROWS = (2, 0, 1)
+LAST_ROW = 3
+CHUNKS = (1024, 1024, 1024, 512, 512)
+VECTOR_CHUNK = 2
+PIECES = ((0, 0, 256), (0, 256, 256), (1, 0, 512))
+SCATTERS = ((0, 256), (256, 768))
+
+
+def entries(lst, first, count):
+    return lst[:, first // 16 : (first + count) // 16]
+
+
+def tile_picked_kvput_none_e_kernel(tc, xT, mem, w1_words, w1_scales, offs, slot, out):
+    nc = tc.nc
+    x_rows = xT.rearrange("(p j) t -> p j t", j=PACK)
+
+    with ExitStack() as ctx:
+        keep = ctx.enter_context(tc.tile_pool(name="keep", bufs=1))
+        psum = ctx.enter_context(tc.psum_pool(name="psum", bufs=1))
+
+        offs_sb = keep.tile([P, S // 16], U16, name="offs_sb")
+        slot_sb = keep.tile([P, S // 16], U16, name="slot_sb")
+        raw = [keep.tile([P, T], F32, name=f"raw{j}") for j in range(PACK)]
+        last_bf16 = keep.tile([P, T], BF16, name="last_bf16")
+        cache = keep.tile([P, U], F32, name="cache")
+        w_codes = keep.tile([P, 2 * N], U8, name="w_codes", align_bytes=64)
+        w_scales = keep.tile([P, N], U8, name="w_scales", align_bytes=64)
+        grouped = [keep.tile([P, HALF, PACK], BF16, name=f"grouped{h}", align_bytes=64) for h in range(2)]
+        y = keep.tile([P, S], F32, name="y")
+
+        nc.sync.dma_start(raw[EARLY_ROWS[0]][:], x_rows[:, EARLY_ROWS[0], :])
+        nc.sync.dma_start(offs_sb[:], offs)
+        nc.sync.dma_start(slot_sb[:], slot)
+        for j in EARLY_ROWS[1:]:
+            nc.sync.dma_start(raw[j][:], x_rows[:, j, :])
+        spans = []
+        first = 0
+        for width in CHUNKS:
+            spans.append(slice(first, first + width))
+            first = first + width
+        for cols in spans:
+            nc.sync.dma_start(raw[LAST_ROW][:, cols], x_rows[:, LAST_ROW, cols])
+        nc.sync.dma_start(cache[:], mem)
+
+        nc.gpsimd.memset(w_scales[:].bitcast(I32), 0)
+        nc.gpsimd.dma_start(w_codes[:].bitcast(I32), w1_words[0].bitcast(I32))
+        for q in range(4):
+            nc.gpsimd.dma_start(w_scales[32 * q : 32 * q + 4, :].bitcast(I32), w1_scales[0, 4 * q : 4 * q + 4, :].bitcast(I32))
+
+        for j in EARLY_ROWS:
+            for h in range(2):
+                nc.vector.tensor_copy(grouped[h][:, :, j], raw[j][:].indirect(entries(offs_sb, h * HALF, HALF)))
+
+        for c, cols in enumerate(spans):
+            if c == VECTOR_CHUNK:
+                nc.vector.tensor_copy(last_bf16[:, cols], raw[LAST_ROW][:, cols])
+            else:
+                nc.scalar.activation(last_bf16[:, cols], raw[LAST_ROW][:, cols], COPY)
+
+        nc.vector.tensor_copy(grouped[0][:, :, LAST_ROW], raw[LAST_ROW][:].indirect(entries(offs_sb, 0, HALF)))
+        nc.scalar.activation(grouped[1][:, :, LAST_ROW], last_bf16[:].indirect(entries(offs_sb, HALF, HALF)), COPY)
+
+        for i, (h, start, width) in enumerate(PIECES):
+            codes = keep.tile([P, width], U32, name=f"codes{i}", align_bytes=64)
+            scales = keep.tile([P, width], U8, name=f"scales{i}", align_bytes=64)
+            nc.vector.quantize_mx(
+                out=codes[:].bitcast(FP8X4),
+                scales=scales[:],
+                in_=grouped[h][:, start : start + width, :].rearrange("p n j -> p (n j)"),
+            )
+            acc = psum.tile([N, width], F32, name=f"acc{i}")
+            nc.tensor.matmul_mx(
+                out=acc[:],
+                lhsT=w_codes[:].bitcast(FP4X4),
+                lhsT_scale=w_scales[:],
+                rhs=codes[:].bitcast(FP8X4),
+                rhs_scale=scales[:],
+                start=True,
+                stop=True,
+            )
+            at = h * HALF + start
+            nc.scalar.copy(y[:, at : at + width], acc[:])
+
+        for at, width in SCATTERS:
+            nc.vector.tensor_copy(cache[:].indirect(entries(slot_sb, at, width)), y[:, at : at + width])
+
+        nc.sync.dma_start(out, cache[:])

@@ -20,10 +20,9 @@ PACK = 4
 HALF = S // 2
 EARLY_ROWS = (2, 0, 1)
 LAST_ROW = 3
-CHUNKS = (1024, 1024, 1024, 512, 512)
-VECTOR_CHUNK = 2
-PIECES = ((0, 0, 256), (0, 256, 256), (1, 0, 512))
-SCATTERS = ((0, 256), (256, 768))
+CHUNKS = (1024, 1280, 1024, 512, 256)
+VECTOR_CHUNKS = (2, 3)
+WIDTH = 256
 
 
 def entries(lst, first, count):
@@ -46,13 +45,18 @@ def tile_picked_kvput_none_e_kernel(tc, xT, mem, w1_words, w1_scales, offs, slot
         w_codes = keep.tile([P, 2 * N], U8, name="w_codes", align_bytes=64)
         w_scales = keep.tile([P, N], U8, name="w_scales", align_bytes=64)
         grouped = [keep.tile([P, HALF, PACK], BF16, name=f"grouped{h}", align_bytes=64) for h in range(2)]
-        y = keep.tile([P, S], F32, name="y")
+        y_first = grouped[1][:].rearrange("p n j -> p (n j)")[:, 0 : 2 * WIDTH].bitcast(F32)
+        y_rest = keep.tile([P, S - WIDTH], F32, name="y_rest")
 
+        nc.gpsimd.memset(w_scales[:].bitcast(I32), 0)
         nc.sync.dma_start(raw[EARLY_ROWS[0]][:], x_rows[:, EARLY_ROWS[0], :])
         nc.sync.dma_start(offs_sb[:], offs)
+        nc.sync.dma_start(raw[EARLY_ROWS[1]][:], x_rows[:, EARLY_ROWS[1], :])
         nc.sync.dma_start(slot_sb[:], slot)
-        for j in EARLY_ROWS[1:]:
-            nc.sync.dma_start(raw[j][:], x_rows[:, j, :])
+        nc.sync.dma_start(w_codes[:].bitcast(I32), w1_words[0].bitcast(I32))
+        for q in range(4):
+            nc.sync.dma_start(w_scales[32 * q : 32 * q + 4, :].bitcast(I32), w1_scales[0, 4 * q : 4 * q + 4, :].bitcast(I32))
+        nc.sync.dma_start(raw[EARLY_ROWS[2]][:], x_rows[:, EARLY_ROWS[2], :])
         spans = []
         first = 0
         for width in CHUNKS:
@@ -62,17 +66,12 @@ def tile_picked_kvput_none_e_kernel(tc, xT, mem, w1_words, w1_scales, offs, slot
             nc.sync.dma_start(raw[LAST_ROW][:, cols], x_rows[:, LAST_ROW, cols])
         nc.sync.dma_start(cache[:], mem)
 
-        nc.gpsimd.memset(w_scales[:].bitcast(I32), 0)
-        nc.gpsimd.dma_start(w_codes[:].bitcast(I32), w1_words[0].bitcast(I32))
-        for q in range(4):
-            nc.gpsimd.dma_start(w_scales[32 * q : 32 * q + 4, :].bitcast(I32), w1_scales[0, 4 * q : 4 * q + 4, :].bitcast(I32))
-
         for j in EARLY_ROWS:
             for h in range(2):
                 nc.vector.tensor_copy(grouped[h][:, :, j], raw[j][:].indirect(entries(offs_sb, h * HALF, HALF)))
 
         for c, cols in enumerate(spans):
-            if c == VECTOR_CHUNK:
+            if c in VECTOR_CHUNKS:
                 nc.vector.tensor_copy(last_bf16[:, cols], raw[LAST_ROW][:, cols])
             else:
                 nc.scalar.activation(last_bf16[:, cols], raw[LAST_ROW][:, cols], COPY)
@@ -80,15 +79,20 @@ def tile_picked_kvput_none_e_kernel(tc, xT, mem, w1_words, w1_scales, offs, slot
         nc.vector.tensor_copy(grouped[0][:, :, LAST_ROW], raw[LAST_ROW][:].indirect(entries(offs_sb, 0, HALF)))
         nc.scalar.activation(grouped[1][:, :, LAST_ROW], last_bf16[:].indirect(entries(offs_sb, HALF, HALF)), COPY)
 
-        for i, (h, start, width) in enumerate(PIECES):
-            codes = keep.tile([P, width], U32, name=f"codes{i}", align_bytes=64)
-            scales = keep.tile([P, width], U8, name=f"scales{i}", align_bytes=64)
+        quantised = []
+        for i in range(S // WIDTH):
+            h, start = divmod(i * WIDTH, HALF)
+            codes = keep.tile([P, WIDTH], U32, name=f"codes{i}", align_bytes=64)
+            scales = keep.tile([P, WIDTH], U8, name=f"scales{i}", align_bytes=64)
             nc.vector.quantize_mx(
                 out=codes[:].bitcast(FP8X4),
                 scales=scales[:],
-                in_=grouped[h][:, start : start + width, :].rearrange("p n j -> p (n j)"),
+                in_=grouped[h][:, start : start + WIDTH, :].rearrange("p n j -> p (n j)"),
             )
-            acc = psum.tile([N, width], F32, name=f"acc{i}")
+            quantised.append((codes, scales))
+
+        for i, (codes, scales) in enumerate(quantised):
+            acc = psum.tile([N, WIDTH], F32, name=f"acc{i}")
             nc.tensor.matmul_mx(
                 out=acc[:],
                 lhsT=w_codes[:].bitcast(FP4X4),
@@ -98,10 +102,9 @@ def tile_picked_kvput_none_e_kernel(tc, xT, mem, w1_words, w1_scales, offs, slot
                 start=True,
                 stop=True,
             )
-            at = h * HALF + start
-            nc.scalar.copy(y[:, at : at + width], acc[:])
+            nc.scalar.copy(y_first if i == 0 else y_rest[:, (i - 1) * WIDTH : i * WIDTH], acc[:])
 
-        for at, width in SCATTERS:
-            nc.vector.tensor_copy(cache[:].indirect(entries(slot_sb, at, width)), y[:, at : at + width])
+        nc.vector.tensor_copy(cache[:].indirect(entries(slot_sb, 0, WIDTH)), y_first)
+        nc.vector.tensor_copy(cache[:].indirect(entries(slot_sb, WIDTH, S - WIDTH)), y_rest[:])
 
         nc.sync.dma_start(out, cache[:])

@@ -23,6 +23,7 @@ LAST_ROW = 3
 CHUNKS = (1024, 1280, 1024, 512, 256)
 VECTOR_CHUNKS = (2, 3)
 WIDTH = 256
+PIECES = ((0, 256), (256, 256), (512, 512))
 
 
 def entries(lst, first, count):
@@ -40,23 +41,19 @@ def tile_picked_kvput_none_e_kernel(tc, xT, mem, w1_words, w1_scales, offs, slot
         offs_sb = keep.tile([P, S // 16], U16, name="offs_sb")
         slot_sb = keep.tile([P, S // 16], U16, name="slot_sb")
         raw = [keep.tile([P, T], F32, name=f"raw{j}") for j in range(PACK)]
-        last_bf16 = keep.tile([P, T], BF16, name="last_bf16")
+        last_bf16 = keep.tile([P, T], BF16, name="last_bf16", tag="shared")
         cache = keep.tile([P, U], F32, name="cache")
         w_codes = keep.tile([P, 2 * N], U8, name="w_codes", align_bytes=64)
         w_scales = keep.tile([P, N], U8, name="w_scales", align_bytes=64)
         grouped = [keep.tile([P, HALF, PACK], BF16, name=f"grouped{h}", align_bytes=64) for h in range(2)]
-        y_first = grouped[1][:].rearrange("p n j -> p (n j)")[:, 0 : 2 * WIDTH].bitcast(F32)
-        y_rest = keep.tile([P, S - WIDTH], F32, name="y_rest")
 
-        nc.gpsimd.memset(w_scales[:].bitcast(I32), 0)
+        nc.vector.memset(w_scales[:].bitcast(I32), 0)
         nc.sync.dma_start(raw[EARLY_ROWS[0]][:], x_rows[:, EARLY_ROWS[0], :])
         nc.sync.dma_start(offs_sb[:], offs)
-        nc.sync.dma_start(raw[EARLY_ROWS[1]][:], x_rows[:, EARLY_ROWS[1], :])
-        nc.sync.dma_start(slot_sb[:], slot)
-        nc.sync.dma_start(w_codes[:].bitcast(I32), w1_words[0].bitcast(I32))
         for q in range(4):
             nc.sync.dma_start(w_scales[32 * q : 32 * q + 4, :].bitcast(I32), w1_scales[0, 4 * q : 4 * q + 4, :].bitcast(I32))
-        nc.sync.dma_start(raw[EARLY_ROWS[2]][:], x_rows[:, EARLY_ROWS[2], :])
+        for j in EARLY_ROWS[1:]:
+            nc.sync.dma_start(raw[j][:], x_rows[:, j, :])
         spans = []
         first = 0
         for width in CHUNKS:
@@ -64,7 +61,9 @@ def tile_picked_kvput_none_e_kernel(tc, xT, mem, w1_words, w1_scales, offs, slot
             first = first + width
         for cols in spans:
             nc.sync.dma_start(raw[LAST_ROW][:, cols], x_rows[:, LAST_ROW, cols])
+        nc.sync.dma_start(w_codes[:].bitcast(I32), w1_words[0].bitcast(I32))
         nc.sync.dma_start(cache[:], mem)
+        nc.sync.dma_start(slot_sb[:], slot)
 
         for j in EARLY_ROWS:
             for h in range(2):
@@ -79,20 +78,22 @@ def tile_picked_kvput_none_e_kernel(tc, xT, mem, w1_words, w1_scales, offs, slot
         nc.vector.tensor_copy(grouped[0][:, :, LAST_ROW], raw[LAST_ROW][:].indirect(entries(offs_sb, 0, HALF)))
         nc.scalar.activation(grouped[1][:, :, LAST_ROW], last_bf16[:].indirect(entries(offs_sb, HALF, HALF)), COPY)
 
+        y = keep.tile([P, S], F32, name="y", tag="shared")
         quantised = []
-        for i in range(S // WIDTH):
-            h, start = divmod(i * WIDTH, HALF)
-            codes = keep.tile([P, WIDTH], U32, name=f"codes{i}", align_bytes=64)
-            scales = keep.tile([P, WIDTH], U8, name=f"scales{i}", align_bytes=64)
+        for i, (at, width) in enumerate(PIECES):
+            h, start = divmod(at, HALF)
+            codes = keep.tile([P, width], U32, name=f"codes{i}", align_bytes=64)
+            scales = keep.tile([P, width], U8, name=f"scales{i}", align_bytes=64)
             nc.vector.quantize_mx(
                 out=codes[:].bitcast(FP8X4),
                 scales=scales[:],
-                in_=grouped[h][:, start : start + WIDTH, :].rearrange("p n j -> p (n j)"),
+                in_=grouped[h][:, start : start + width, :].rearrange("p n j -> p (n j)"),
             )
             quantised.append((codes, scales))
 
-        for i, (codes, scales) in enumerate(quantised):
-            acc = psum.tile([N, WIDTH], F32, name=f"acc{i}")
+        for i, (at, width) in enumerate(PIECES):
+            codes, scales = quantised[i]
+            acc = psum.tile([N, width], F32, name=f"acc{i}")
             nc.tensor.matmul_mx(
                 out=acc[:],
                 lhsT=w_codes[:].bitcast(FP4X4),
@@ -102,9 +103,9 @@ def tile_picked_kvput_none_e_kernel(tc, xT, mem, w1_words, w1_scales, offs, slot
                 start=True,
                 stop=True,
             )
-            nc.scalar.copy(y_first if i == 0 else y_rest[:, (i - 1) * WIDTH : i * WIDTH], acc[:])
+            nc.scalar.copy(y[:, at : at + width], acc[:])
 
-        nc.vector.tensor_copy(cache[:].indirect(entries(slot_sb, 0, WIDTH)), y_first)
-        nc.vector.tensor_copy(cache[:].indirect(entries(slot_sb, WIDTH, S - WIDTH)), y_rest[:])
+        nc.vector.tensor_copy(cache[:].indirect(entries(slot_sb, 0, WIDTH)), y[:, 0:WIDTH])
+        nc.vector.tensor_copy(cache[:].indirect(entries(slot_sb, WIDTH, S - WIDTH)), y[:, WIDTH:S])
 
         nc.sync.dma_start(out, cache[:])

@@ -50,8 +50,6 @@ def tile_picked_kvput_none_e_kernel(tc, xT, mem, w1_words, w1_scales, offs, slot
         nc.vector.memset(w_scales[:].bitcast(I32), 0)
         nc.sync.dma_start(raw[EARLY_ROWS[0]][:], x_rows[:, EARLY_ROWS[0], :])
         nc.sync.dma_start(offs_sb[:], offs)
-        for q in range(4):
-            nc.sync.dma_start(w_scales[32 * q : 32 * q + 4, :].bitcast(I32), w1_scales[0, 4 * q : 4 * q + 4, :].bitcast(I32))
         for j in EARLY_ROWS[1:]:
             nc.sync.dma_start(raw[j][:], x_rows[:, j, :])
         spans = []
@@ -61,8 +59,11 @@ def tile_picked_kvput_none_e_kernel(tc, xT, mem, w1_words, w1_scales, offs, slot
             first = first + width
         for cols in spans:
             nc.sync.dma_start(raw[LAST_ROW][:, cols], x_rows[:, LAST_ROW, cols])
+        nc.sync.dma_start(cache[:, : U // 2], mem[:, : U // 2])
         nc.sync.dma_start(w_codes[:].bitcast(I32), w1_words[0].bitcast(I32))
-        nc.sync.dma_start(cache[:], mem)
+        for q in range(4):
+            nc.sync.dma_start(w_scales[32 * q : 32 * q + 4, :].bitcast(I32), w1_scales[0, 4 * q : 4 * q + 4, :].bitcast(I32))
+        nc.sync.dma_start(cache[:, U // 2 :], mem[:, U // 2 :])
         nc.sync.dma_start(slot_sb[:], slot)
 
         for j in EARLY_ROWS:

@@ -23,7 +23,7 @@ LAST_ROW = 3
 CHUNKS = (1024, 1280, 1024, 512, 256)
 VECTOR_CHUNKS = (2, 3)
 WIDTH = 256
-PIECES = ((0, 256), (256, 256), (512, 512))
+PIECES = ((0, 128), (128, 128), (256, 256), (512, 512))
 
 
 def entries(lst, first, count):

@@ -20,10 +20,10 @@ PACK = 4
 HALF = S // 2
 EARLY_ROWS = (2, 0, 1)
 LAST_ROW = 3
-CHUNKS = (1024, 1280, 1024, 512, 256)
-VECTOR_CHUNKS = (2, 3)
+CHUNKS = (1088, 1344, 1024, 384, 256)
+VECTOR_CHUNKS = (2,)
 WIDTH = 256
-PIECES = ((0, 128), (128, 128), (256, 256), (512, 512))
+PIECES = ((0, 128), (128, 128), (256, 256), (512, 256), (768, 256))
 
 
 def entries(lst, first, count):
@@ -63,8 +63,8 @@ def tile_picked_kvput_none_e_kernel(tc, xT, mem, w1_words, w1_scales, offs, slot
         nc.sync.dma_start(w_codes[:].bitcast(I32), w1_words[0].bitcast(I32))
         for q in range(4):
             nc.sync.dma_start(w_scales[32 * q : 32 * q + 4, :].bitcast(I32), w1_scales[0, 4 * q : 4 * q + 4, :].bitcast(I32))
-        nc.sync.dma_start(cache[:, U // 2 :], mem[:, U // 2 :])
         nc.sync.dma_start(slot_sb[:], slot)
+        nc.sync.dma_start(cache[:, U // 2 :], mem[:, U // 2 :])
 
         for j in EARLY_ROWS:
             for h in range(2):

@@ -20,10 +20,10 @@ PACK = 4
 HALF = S // 2
 EARLY_ROWS = (2, 0, 1)
 LAST_ROW = 3
-CHUNKS = (1088, 1344, 1024, 384, 256)
-VECTOR_CHUNKS = (2,)
-WIDTH = 256
-PIECES = ((0, 128), (128, 128), (256, 256), (512, 256), (768, 256))
+CHUNKS = (1152, 1408, 896, 384, 256)
+VECTOR_CHUNKS = (2, 3)
+WIDTH = 128
+PIECES = ((0, 128), (128, 128), (256, 256), (512, 256), (768, 128), (896, 128))
 
 
 def entries(lst, first, count):
@@ -47,7 +47,9 @@ def tile_picked_kvput_none_e_kernel(tc, xT, mem, w1_words, w1_scales, offs, slot
         w_scales = keep.tile([P, N], U8, name="w_scales", align_bytes=64)
         grouped = [keep.tile([P, HALF, PACK], BF16, name=f"grouped{h}", align_bytes=64) for h in range(2)]
 
+        zeros = keep.tile([P, WIDTH], F32, name="zeros")
         nc.vector.memset(w_scales[:].bitcast(I32), 0)
+        nc.vector.memset(zeros[:], 0.0)
         nc.sync.dma_start(raw[EARLY_ROWS[0]][:], x_rows[:, EARLY_ROWS[0], :])
         nc.sync.dma_start(offs_sb[:], offs)
         for j in EARLY_ROWS[1:]:
@@ -106,7 +108,7 @@ def tile_picked_kvput_none_e_kernel(tc, xT, mem, w1_words, w1_scales, offs, slot
             )
             nc.scalar.copy(y[:, at : at + width], acc[:])
 
-        nc.vector.tensor_copy(cache[:].indirect(entries(slot_sb, 0, WIDTH)), y[:, 0:WIDTH])
+        nc.vector.tensor_tensor(cache[:].indirect(entries(slot_sb, 0, WIDTH)), y[:, 0:WIDTH], zeros[:], mybir.AluOpType.add)
         nc.vector.tensor_copy(cache[:].indirect(entries(slot_sb, WIDTH, S - WIDTH)), y[:, WIDTH:S])
 
         nc.sync.dma_start(out, cache[:])

@@ -23,7 +23,8 @@ LAST_ROW = 3
 CHUNKS = (1152, 1408, 896, 384, 256)
 VECTOR_CHUNKS = (2, 3)
 WIDTH = 128
-PIECES = ((0, 128), (128, 128), (256, 256), (512, 256), (768, 128), (896, 128))
+MEM_SPLIT = 1280
+PIECES = ((0, 128), (128, 128), (256, 256), (512, 128), (640, 128), (768, 128), (896, 128))
 
 
 def entries(lst, first, count):
@@ -61,12 +62,12 @@ def tile_picked_kvput_none_e_kernel(tc, xT, mem, w1_words, w1_scales, offs, slot
             first = first + width
         for cols in spans:
             nc.sync.dma_start(raw[LAST_ROW][:, cols], x_rows[:, LAST_ROW, cols])
-        nc.sync.dma_start(cache[:, : U // 2], mem[:, : U // 2])
+        nc.sync.dma_start(cache[:, :MEM_SPLIT], mem[:, :MEM_SPLIT])
         nc.sync.dma_start(w_codes[:].bitcast(I32), w1_words[0].bitcast(I32))
         for q in range(4):
             nc.sync.dma_start(w_scales[32 * q : 32 * q + 4, :].bitcast(I32), w1_scales[0, 4 * q : 4 * q + 4, :].bitcast(I32))
+        nc.sync.dma_start(cache[:, MEM_SPLIT:], mem[:, MEM_SPLIT:])
         nc.sync.dma_start(slot_sb[:], slot)
-        nc.sync.dma_start(cache[:, U // 2 :], mem[:, U // 2 :])
 
         for j in EARLY_ROWS:
             for h in range(2):

@@ -24,7 +24,7 @@ CHUNKS = (1152, 1408, 896, 384, 256)
 VECTOR_CHUNKS = (2, 3)
 WIDTH = 128
 MEM_SPLIT = 1280
-PIECES = ((0, 128), (128, 128), (256, 256), (512, 128), (640, 128), (768, 128), (896, 128))
+FIRST_SCATTER = 128
 
 
 def entries(lst, first, count):
@@ -48,7 +48,7 @@ def tile_picked_kvput_none_e_kernel(tc, xT, mem, w1_words, w1_scales, offs, slot
         w_scales = keep.tile([P, N], U8, name="w_scales", align_bytes=64)
         grouped = [keep.tile([P, HALF, PACK], BF16, name=f"grouped{h}", align_bytes=64) for h in range(2)]
 
-        zeros = keep.tile([P, WIDTH], F32, name="zeros")
+        zeros = keep.tile([P, FIRST_SCATTER], F32, name="zeros")
         nc.vector.memset(w_scales[:].bitcast(I32), 0)
         nc.vector.memset(zeros[:], 0.0)
         nc.sync.dma_start(raw[EARLY_ROWS[0]][:], x_rows[:, EARLY_ROWS[0], :])
@@ -79,24 +79,46 @@ def tile_picked_kvput_none_e_kernel(tc, xT, mem, w1_words, w1_scales, offs, slot
             else:
                 nc.scalar.activation(last_bf16[:, cols], raw[LAST_ROW][:, cols], COPY)
 
-        nc.vector.tensor_copy(grouped[0][:, :, LAST_ROW], raw[LAST_ROW][:].indirect(entries(offs_sb, 0, HALF)))
         nc.scalar.activation(grouped[1][:, :, LAST_ROW], last_bf16[:].indirect(entries(offs_sb, HALF, HALF)), COPY)
 
-        y = keep.tile([P, S], F32, name="y", tag="shared")
+        plain = [keep.tile([P, WIDTH], BF16, name=f"plain{i}") for i in range(HALF // WIDTH)]
         quantised = []
-        for i, (at, width) in enumerate(PIECES):
-            h, start = divmod(at, HALF)
-            codes = keep.tile([P, width], U32, name=f"codes{i}", align_bytes=64)
-            scales = keep.tile([P, width], U8, name=f"scales{i}", align_bytes=64)
+
+        def fetch(i):
+            nc.vector.tensor_copy(plain[i][:], raw[LAST_ROW][:].indirect(entries(offs_sb, i * WIDTH, WIDTH)))
+
+        def weave(i):
+            target = grouped[0][:, i * WIDTH : (i + 1) * WIDTH, LAST_ROW]
+            if i == 0:
+                nc.gpsimd.tensor_scalar(target, plain[i][:], 1.0, 0.0, mybir.AluOpType.mult, mybir.AluOpType.add)
+            else:
+                nc.vector.tensor_copy(target, plain[i][:])
+
+        def quantise(i):
+            h, start = divmod(i * WIDTH, HALF)
+            codes = keep.tile([P, WIDTH], U32, name=f"codes{i}", align_bytes=64)
+            scales = keep.tile([P, WIDTH], U8, name=f"scales{i}", align_bytes=64)
             nc.vector.quantize_mx(
                 out=codes[:].bitcast(FP8X4),
                 scales=scales[:],
-                in_=grouped[h][:, start : start + width, :].rearrange("p n j -> p (n j)"),
+                in_=grouped[h][:, start : start + WIDTH, :].rearrange("p n j -> p (n j)"),
             )
             quantised.append((codes, scales))
 
-        for i, (at, width) in enumerate(PIECES):
-            codes, scales = quantised[i]
+        fetched = len(plain)
+        for step in range(fetched + 2):
+            if step < fetched:
+                fetch(step)
+            if 1 <= step <= fetched:
+                weave(step - 1)
+            if step >= 2:
+                quantise(step - 2)
+        for i in range(fetched, S // WIDTH):
+            quantise(i)
+
+        y = keep.tile([P, S], F32, name="y", tag="shared")
+        for i, (codes, scales) in enumerate(quantised):
+            at, width = i * WIDTH, WIDTH
             acc = psum.tile([N, width], F32, name=f"acc{i}")
             nc.tensor.matmul_mx(
                 out=acc[:],
@@ -109,7 +131,7 @@ def tile_picked_kvput_none_e_kernel(tc, xT, mem, w1_words, w1_scales, offs, slot
             )
             nc.scalar.copy(y[:, at : at + width], acc[:])
 
-        nc.vector.tensor_tensor(cache[:].indirect(entries(slot_sb, 0, WIDTH)), y[:, 0:WIDTH], zeros[:], mybir.AluOpType.add)
-        nc.vector.tensor_copy(cache[:].indirect(entries(slot_sb, WIDTH, S - WIDTH)), y[:, WIDTH:S])
+        nc.vector.tensor_tensor(cache[:].indirect(entries(slot_sb, 0, FIRST_SCATTER)), y[:, :FIRST_SCATTER], zeros[:], mybir.AluOpType.add)
+        nc.vector.tensor_copy(cache[:].indirect(entries(slot_sb, FIRST_SCATTER, S - FIRST_SCATTER)), y[:, FIRST_SCATTER:])
 
         nc.sync.dma_start(out, cache[:])

@@ -21,7 +21,8 @@ HALF = S // 2
 EARLY_ROWS = (2, 0, 1)
 LAST_ROW = 3
 CHUNKS = (1152, 1408, 896, 384, 256)
-VECTOR_CHUNKS = (2, 3)
+VECTOR_CHUNK = 2
+GPSIMD_SHARE = (0, 512, 0, 192, 128)
 WIDTH = 128
 MEM_SPLIT = 1280
 FIRST_SCATTER = 128
@@ -73,11 +74,14 @@ def tile_picked_kvput_none_e_kernel(tc, xT, mem, w1_words, w1_scales, offs, slot
             for h in range(2):
                 nc.vector.tensor_copy(grouped[h][:, :, j], raw[j][:].indirect(entries(offs_sb, h * HALF, HALF)))
 
-        for c, cols in enumerate(spans):
-            if c in VECTOR_CHUNKS:
+        for c, (cols, share) in enumerate(zip(spans, GPSIMD_SHARE)):
+            cut = cols.stop - share
+            if c == VECTOR_CHUNK:
                 nc.vector.tensor_copy(last_bf16[:, cols], raw[LAST_ROW][:, cols])
             else:
-                nc.scalar.activation(last_bf16[:, cols], raw[LAST_ROW][:, cols], COPY)
+                nc.scalar.activation(last_bf16[:, cols.start : cut], raw[LAST_ROW][:, cols.start : cut], COPY)
+            if share:
+                nc.gpsimd.tensor_scalar(last_bf16[:, cut : cols.stop], raw[LAST_ROW][:, cut : cols.stop], 1.0, 0.0, mybir.AluOpType.mult, mybir.AluOpType.add)
 
         nc.scalar.activation(grouped[1][:, :, LAST_ROW], last_bf16[:].indirect(entries(offs_sb, HALF, HALF)), COPY)
 

@@ -20,9 +20,9 @@ PACK = 4
 HALF = S // 2
 EARLY_ROWS = (2, 0, 1)
 LAST_ROW = 3
-CHUNKS = (1152, 1408, 896, 384, 256)
-VECTOR_CHUNK = 2
-GPSIMD_SHARE = (0, 512, 0, 192, 128)
+CHUNKS = (2368, 1216, 512)
+VECTOR_SHARE = (640, 832, 0)
+GPSIMD_SHARE = (576, 0, 256)
 WIDTH = 128
 MEM_SPLIT = 1280
 FIRST_SCATTER = 128
@@ -74,14 +74,13 @@ def tile_picked_kvput_none_e_kernel(tc, xT, mem, w1_words, w1_scales, offs, slot
             for h in range(2):
                 nc.vector.tensor_copy(grouped[h][:, :, j], raw[j][:].indirect(entries(offs_sb, h * HALF, HALF)))
 
-        for c, (cols, share) in enumerate(zip(spans, GPSIMD_SHARE)):
-            cut = cols.stop - share
-            if c == VECTOR_CHUNK:
-                nc.vector.tensor_copy(last_bf16[:, cols], raw[LAST_ROW][:, cols])
-            else:
-                nc.scalar.activation(last_bf16[:, cols.start : cut], raw[LAST_ROW][:, cols.start : cut], COPY)
-            if share:
-                nc.gpsimd.tensor_scalar(last_bf16[:, cut : cols.stop], raw[LAST_ROW][:, cut : cols.stop], 1.0, 0.0, mybir.AluOpType.mult, mybir.AluOpType.add)
+        for cols, on_vector, on_gpsimd in zip(spans, VECTOR_SHARE, GPSIMD_SHARE):
+            lo, hi = cols.start + on_vector, cols.stop - on_gpsimd
+            nc.scalar.activation(last_bf16[:, lo:hi], raw[LAST_ROW][:, lo:hi], COPY)
+            if on_vector:
+                nc.vector.tensor_copy(last_bf16[:, cols.start : lo], raw[LAST_ROW][:, cols.start : lo])
+            if on_gpsimd:
+                nc.gpsimd.tensor_scalar(last_bf16[:, hi : cols.stop], raw[LAST_ROW][:, hi : cols.stop], 1.0, 0.0, mybir.AluOpType.mult, mybir.AluOpType.add)
 
         nc.scalar.activation(grouped[1][:, :, LAST_ROW], last_bf16[:].indirect(entries(offs_sb, HALF, HALF)), COPY)
 

@@ -21,8 +21,9 @@ HALF = S // 2
 EARLY_ROWS = (2, 0, 1)
 LAST_ROW = 3
 CHUNKS = (2368, 1216, 512)
-VECTOR_SHARE = (640, 832, 0)
-GPSIMD_SHARE = (576, 0, 256)
+VECTOR_SHARE = (0, 832, 0)
+GPSIMD_SHARE = (1088, 0, 256)
+FETCHES = (160, 192, 160)
 WIDTH = 128
 MEM_SPLIT = 1280
 FIRST_SCATTER = 128
@@ -84,14 +85,15 @@ def tile_picked_kvput_none_e_kernel(tc, xT, mem, w1_words, w1_scales, offs, slot
 
         nc.scalar.activation(grouped[1][:, :, LAST_ROW], last_bf16[:].indirect(entries(offs_sb, HALF, HALF)), COPY)
 
-        plain = [keep.tile([P, WIDTH], BF16, name=f"plain{i}") for i in range(HALF // WIDTH)]
+        plain = [keep.tile([P, count], BF16, name=f"plain{i}") for i, count in enumerate(FETCHES)]
+        starts = [sum(FETCHES[:i]) for i in range(len(FETCHES))]
         quantised = []
 
         def fetch(i):
-            nc.vector.tensor_copy(plain[i][:], raw[LAST_ROW][:].indirect(entries(offs_sb, i * WIDTH, WIDTH)))
+            nc.vector.tensor_copy(plain[i][:], raw[LAST_ROW][:].indirect(entries(offs_sb, starts[i], FETCHES[i])))
 
         def weave(i):
-            target = grouped[0][:, i * WIDTH : (i + 1) * WIDTH, LAST_ROW]
+            target = grouped[0][:, starts[i] : starts[i] + FETCHES[i], LAST_ROW]
             if i == 0:
                 nc.gpsimd.tensor_scalar(target, plain[i][:], 1.0, 0.0, mybir.AluOpType.mult, mybir.AluOpType.add)
             else:
@@ -108,15 +110,11 @@ def tile_picked_kvput_none_e_kernel(tc, xT, mem, w1_words, w1_scales, offs, slot
             )
             quantised.append((codes, scales))
 
-        fetched = len(plain)
-        for step in range(fetched + 2):
-            if step < fetched:
-                fetch(step)
-            if 1 <= step <= fetched:
-                weave(step - 1)
-            if step >= 2:
-                quantise(step - 2)
-        for i in range(fetched, S // WIDTH):
+        for i in range(len(FETCHES)):
+            fetch(i)
+        for i in range(len(FETCHES)):
+            weave(i)
+        for i in range(S // WIDTH):
             quantise(i)
 
         y = keep.tile([P, S], F32, name="y", tag="shared")

@@ -20,13 +20,8 @@ PACK = 4
 HALF = S // 2
 EARLY_ROWS = (2, 0, 1)
 LAST_ROW = 3
-CHUNKS = (2368, 1216, 512)
-VECTOR_SHARE = (0, 832, 0)
-GPSIMD_SHARE = (1088, 0, 256)
-FETCHES = (160, 192, 160)
-WIDTH = 128
-MEM_SPLIT = 1280
-FIRST_SCATTER = 128
+PIECE = 256
+SCALAR_SCATTERS = (384,)
 
 
 def entries(lst, first, count):
@@ -44,83 +39,57 @@ def tile_picked_kvput_none_e_kernel(tc, xT, mem, w1_words, w1_scales, offs, slot
         offs_sb = keep.tile([P, S // 16], U16, name="offs_sb")
         slot_sb = keep.tile([P, S // 16], U16, name="slot_sb")
         raw = [keep.tile([P, T], F32, name=f"raw{j}") for j in range(PACK)]
-        last_bf16 = keep.tile([P, T], BF16, name="last_bf16", tag="shared")
         cache = keep.tile([P, U], F32, name="cache")
         w_codes = keep.tile([P, 2 * N], U8, name="w_codes", align_bytes=64)
         w_scales = keep.tile([P, N], U8, name="w_scales", align_bytes=64)
-        grouped = [keep.tile([P, HALF, PACK], BF16, name=f"grouped{h}", align_bytes=64) for h in range(2)]
+        grouped = keep.tile([P, S, PACK], BF16, name="grouped", align_bytes=64)
+        y = keep.tile([P, S], F32, name="y")
 
-        zeros = keep.tile([P, FIRST_SCATTER], F32, name="zeros")
         nc.vector.memset(w_scales[:].bitcast(I32), 0)
-        nc.vector.memset(zeros[:], 0.0)
         nc.sync.dma_start(raw[EARLY_ROWS[0]][:], x_rows[:, EARLY_ROWS[0], :])
         nc.sync.dma_start(offs_sb[:], offs)
-        for j in EARLY_ROWS[1:]:
+        for j in EARLY_ROWS[1:] + (LAST_ROW,):
             nc.sync.dma_start(raw[j][:], x_rows[:, j, :])
-        spans = []
-        first = 0
-        for width in CHUNKS:
-            spans.append(slice(first, first + width))
-            first = first + width
-        for cols in spans:
-            nc.sync.dma_start(raw[LAST_ROW][:, cols], x_rows[:, LAST_ROW, cols])
-        nc.sync.dma_start(cache[:, :MEM_SPLIT], mem[:, :MEM_SPLIT])
         nc.sync.dma_start(w_codes[:].bitcast(I32), w1_words[0].bitcast(I32))
         for q in range(4):
             nc.sync.dma_start(w_scales[32 * q : 32 * q + 4, :].bitcast(I32), w1_scales[0, 4 * q : 4 * q + 4, :].bitcast(I32))
-        nc.sync.dma_start(cache[:, MEM_SPLIT:], mem[:, MEM_SPLIT:])
         nc.sync.dma_start(slot_sb[:], slot)
+        nc.sync.dma_start(cache[:], mem)
 
         for j in EARLY_ROWS:
             for h in range(2):
-                nc.vector.tensor_copy(grouped[h][:, :, j], raw[j][:].indirect(entries(offs_sb, h * HALF, HALF)))
+                picked = raw[j][:].indirect(entries(offs_sb, h * HALF, HALF))
+                target = grouped[:, h * HALF : (h + 1) * HALF, j]
+                if (j, h) == (EARLY_ROWS[0], 1):
+                    early = keep.tile([P, HALF], BF16, name="early")
+                    nc.scalar.activation(early[:], picked, COPY)
+                    nc.vector.tensor_copy(target, early[:])
+                else:
+                    nc.vector.tensor_copy(target, picked)
 
-        for cols, on_vector, on_gpsimd in zip(spans, VECTOR_SHARE, GPSIMD_SHARE):
-            lo, hi = cols.start + on_vector, cols.stop - on_gpsimd
-            nc.scalar.activation(last_bf16[:, lo:hi], raw[LAST_ROW][:, lo:hi], COPY)
+        short = PIECE // 2
+        plain = dict()
+
+        def fetch(at, count, on_vector, tag):
+            plain.setdefault(at, keep.tile([P, count], BF16, name=f"plain{at}", tag=tag))
+            picked = raw[LAST_ROW][:].indirect(entries(offs_sb, at, count))
             if on_vector:
-                nc.vector.tensor_copy(last_bf16[:, cols.start : lo], raw[LAST_ROW][:, cols.start : lo])
-            if on_gpsimd:
-                nc.gpsimd.tensor_scalar(last_bf16[:, hi : cols.stop], raw[LAST_ROW][:, hi : cols.stop], 1.0, 0.0, mybir.AluOpType.mult, mybir.AluOpType.add)
-
-        nc.scalar.activation(grouped[1][:, :, LAST_ROW], last_bf16[:].indirect(entries(offs_sb, HALF, HALF)), COPY)
-
-        plain = [keep.tile([P, count], BF16, name=f"plain{i}") for i, count in enumerate(FETCHES)]
-        starts = [sum(FETCHES[:i]) for i in range(len(FETCHES))]
-        quantised = []
-
-        def fetch(i):
-            nc.vector.tensor_copy(plain[i][:], raw[LAST_ROW][:].indirect(entries(offs_sb, starts[i], FETCHES[i])))
-
-        def weave(i):
-            target = grouped[0][:, starts[i] : starts[i] + FETCHES[i], LAST_ROW]
-            if i == 0:
-                nc.gpsimd.tensor_scalar(target, plain[i][:], 1.0, 0.0, mybir.AluOpType.mult, mybir.AluOpType.add)
+                nc.vector.tensor_copy(plain[at][:], picked)
             else:
-                nc.vector.tensor_copy(target, plain[i][:])
+                nc.scalar.activation(plain[at][:], picked, COPY)
 
-        def quantise(i):
-            h, start = divmod(i * WIDTH, HALF)
-            codes = keep.tile([P, WIDTH], U32, name=f"codes{i}", align_bytes=64)
-            scales = keep.tile([P, WIDTH], U8, name=f"scales{i}", align_bytes=64)
+        def weave(at, count):
+            nc.vector.tensor_copy(grouped[:, at : at + count, LAST_ROW], plain[at][:])
+
+        def project(at, width, copy):
+            codes = keep.tile([P, width], U32, name=f"codes{at}", align_bytes=64)
+            scales = keep.tile([P, width], U8, name=f"scales{at}", align_bytes=64)
             nc.vector.quantize_mx(
                 out=codes[:].bitcast(FP8X4),
                 scales=scales[:],
-                in_=grouped[h][:, start : start + WIDTH, :].rearrange("p n j -> p (n j)"),
+                in_=grouped[:, at : at + width, :].rearrange("p n j -> p (n j)"),
             )
-            quantised.append((codes, scales))
-
-        for i in range(len(FETCHES)):
-            fetch(i)
-        for i in range(len(FETCHES)):
-            weave(i)
-        for i in range(S // WIDTH):
-            quantise(i)
-
-        y = keep.tile([P, S], F32, name="y", tag="shared")
-        for i, (codes, scales) in enumerate(quantised):
-            at, width = i * WIDTH, WIDTH
-            acc = psum.tile([N, width], F32, name=f"acc{i}")
+            acc = psum.tile([N, width], F32, name=f"acc{at}")
             nc.tensor.matmul_mx(
                 out=acc[:],
                 lhsT=w_codes[:].bitcast(FP4X4),
@@ -130,9 +99,28 @@ def tile_picked_kvput_none_e_kernel(tc, xT, mem, w1_words, w1_scales, offs, slot
                 start=True,
                 stop=True,
             )
-            nc.scalar.copy(y[:, at : at + width], acc[:])
+            copy(y[:, at : at + width], acc[:])
 
-        nc.vector.tensor_tensor(cache[:].indirect(entries(slot_sb, 0, FIRST_SCATTER)), y[:, :FIRST_SCATTER], zeros[:], mybir.AluOpType.add)
-        nc.vector.tensor_copy(cache[:].indirect(entries(slot_sb, FIRST_SCATTER, S - FIRST_SCATTER)), y[:, FIRST_SCATTER:])
+        lead, last = 3 * short, S - PIECE
+        fetch(0, short, True, "a")
+        fetch(short, short, False, "b")
+        fetch(2 * short, short, False, "c")
+        fetch(lead, last - lead, False, "d")
+        for at in range(0, lead, short):
+            weave(at, short)
+        for at in range(0, lead, short):
+            project(at, short, nc.scalar.copy)
+        fetch(last, PIECE, True, "c")
+        weave(lead, last - lead)
+        weave(last, PIECE)
+        project(lead, short, nc.vector.tensor_copy)
+        project(HALF, PIECE, nc.vector.tensor_copy)
+        project(last, PIECE, nc.vector.tensor_copy)
+
+        at = 0
+        for count in SCALAR_SCATTERS:
+            nc.scalar.activation(cache[:].indirect(entries(slot_sb, at, count)), y[:, at : at + count], COPY)
+            at = at + count
+        nc.vector.tensor_copy(cache[:].indirect(entries(slot_sb, at, S - at)), y[:, at:])
 
         nc.sync.dma_start(out, cache[:])

@@ -81,27 +81,30 @@ def tile_picked_kvput_none_e_kernel(tc, xT, mem, w1_words, w1_scales, offs, slot
         def weave(at, count):
             nc.vector.tensor_copy(grouped[:, at : at + count, LAST_ROW], plain[at][:])
 
-        def project(at, width, copy):
-            codes = keep.tile([P, width], U32, name=f"codes{at}", align_bytes=64)
-            scales = keep.tile([P, width], U8, name=f"scales{at}", align_bytes=64)
-            nc.vector.quantize_mx(
-                out=codes[:].bitcast(FP8X4),
-                scales=scales[:],
-                in_=grouped[:, at : at + width, :].rearrange("p n j -> p (n j)"),
-            )
-            acc = psum.tile([N, width], F32, name=f"acc{at}")
-            nc.tensor.matmul_mx(
-                out=acc[:],
-                lhsT=w_codes[:].bitcast(FP4X4),
-                lhsT_scale=w_scales[:],
-                rhs=codes[:].bitcast(FP8X4),
-                rhs_scale=scales[:],
-                start=True,
-                stop=True,
-            )
-            copy(y[:, at : at + width], acc[:])
+        def project(first, widths, copy):
+            acc = psum.tile([N, sum(widths)], F32, name=f"acc{first}")
+            at = first
+            for width in widths:
+                codes = keep.tile([P, width], U32, name=f"codes{at}", align_bytes=64)
+                scales = keep.tile([P, width], U8, name=f"scales{at}", align_bytes=64)
+                nc.vector.quantize_mx(
+                    out=codes[:].bitcast(FP8X4),
+                    scales=scales[:],
+                    in_=grouped[:, at : at + width, :].rearrange("p n j -> p (n j)"),
+                )
+                nc.tensor.matmul_mx(
+                    out=acc[:, at - first : at - first + width],
+                    lhsT=w_codes[:].bitcast(FP4X4),
+                    lhsT_scale=w_scales[:],
+                    rhs=codes[:].bitcast(FP8X4),
+                    rhs_scale=scales[:],
+                    start=True,
+                    stop=True,
+                )
+                at = at + width
+            copy(y[:, first:at], acc[:])
 
-        lead, last = 3 * short, S - PIECE
+        lead, last = 3 * short, S - 192
         fetch(0, short, True, "a")
         fetch(short, short, False, "b")
         fetch(2 * short, short, False, "c")
@@ -109,13 +112,13 @@ def tile_picked_kvput_none_e_kernel(tc, xT, mem, w1_words, w1_scales, offs, slot
         for at in range(0, lead, short):
             weave(at, short)
         for at in range(0, lead, short):
-            project(at, short, nc.scalar.copy)
-        fetch(last, PIECE, True, "c")
+            project(at, (short,), nc.scalar.copy)
+        fetch(last, S - last, True, "c")
         weave(lead, last - lead)
-        weave(last, PIECE)
-        project(lead, short, nc.vector.tensor_copy)
-        project(HALF, PIECE, nc.vector.tensor_copy)
-        project(last, PIECE, nc.vector.tensor_copy)
+        weave(last, S - last)
+        project(lead, (PIECE,), nc.vector.tensor_copy)
+        project(lead + PIECE, (PIECE,), nc.vector.tensor_copy)
+        project(lead + HALF, (short,), nc.vector.tensor_copy)
 
         at = 0
         for count in SCALAR_SCATTERS:

@@ -48,13 +48,14 @@ def tile_picked_kvput_none_e_kernel(tc, xT, mem, w1_words, w1_scales, offs, slot
         nc.vector.memset(w_scales[:].bitcast(I32), 0)
         nc.sync.dma_start(raw[EARLY_ROWS[0]][:], x_rows[:, EARLY_ROWS[0], :])
         nc.sync.dma_start(offs_sb[:], offs)
-        for j in EARLY_ROWS[1:] + (LAST_ROW,):
+        for j in EARLY_ROWS[1:]:
             nc.sync.dma_start(raw[j][:], x_rows[:, j, :])
-        nc.sync.dma_start(w_codes[:].bitcast(I32), w1_words[0].bitcast(I32))
         for q in range(4):
             nc.sync.dma_start(w_scales[32 * q : 32 * q + 4, :].bitcast(I32), w1_scales[0, 4 * q : 4 * q + 4, :].bitcast(I32))
-        nc.sync.dma_start(slot_sb[:], slot)
+        nc.sync.dma_start(raw[LAST_ROW][:], x_rows[:, LAST_ROW, :])
+        nc.sync.dma_start(w_codes[:].bitcast(I32), w1_words[0].bitcast(I32))
         nc.sync.dma_start(cache[:], mem)
+        nc.sync.dma_start(slot_sb[:], slot)
 
         for j in EARLY_ROWS:
             for h in range(2):

@@ -18,7 +18,7 @@ COPY = mybir.ActivationFunctionType.Copy
 P = 128
 PACK = 4
 HALF = S // 2
-EARLY_ROWS = (2, 0, 1)
+EARLY_ROWS = (0, 1, 2)
 LAST_ROW = 3
 PIECE = 256
 SCALAR_SCATTERS = (384,)
@@ -38,7 +38,8 @@ def tile_picked_kvput_none_e_kernel(tc, xT, mem, w1_words, w1_scales, offs, slot
 
         offs_sb = keep.tile([P, S // 16], U16, name="offs_sb")
         slot_sb = keep.tile([P, S // 16], U16, name="slot_sb")
-        raw = [keep.tile([P, T], F32, name=f"raw{j}") for j in range(PACK)]
+        pair = keep.tile([P, 2, T], F32, name="pair")
+        raw = [pair[:, 0, :], pair[:, 1, :]] + [keep.tile([P, T], F32, name=f"raw{j}")[:] for j in (2, 3)]
         cache = keep.tile([P, U], F32, name="cache")
         w_codes = keep.tile([P, 2 * N], U8, name="w_codes", align_bytes=64)
         w_scales = keep.tile([P, N], U8, name="w_scales", align_bytes=64)
@@ -46,23 +47,22 @@ def tile_picked_kvput_none_e_kernel(tc, xT, mem, w1_words, w1_scales, offs, slot
         y = keep.tile([P, S], F32, name="y")
 
         nc.vector.memset(w_scales[:].bitcast(I32), 0)
-        nc.sync.dma_start(raw[EARLY_ROWS[0]][:], x_rows[:, EARLY_ROWS[0], :])
+        nc.sync.dma_start(pair[:], x_rows[:, 0:2, :])
         nc.sync.dma_start(offs_sb[:], offs)
-        for j in EARLY_ROWS[1:]:
-            nc.sync.dma_start(raw[j][:], x_rows[:, j, :])
+        nc.sync.dma_start(raw[2], x_rows[:, 2, :])
         for q in range(4):
             nc.sync.dma_start(w_scales[32 * q : 32 * q + 4, :].bitcast(I32), w1_scales[0, 4 * q : 4 * q + 4, :].bitcast(I32))
-        nc.sync.dma_start(raw[LAST_ROW][:], x_rows[:, LAST_ROW, :])
+        nc.sync.dma_start(raw[LAST_ROW], x_rows[:, LAST_ROW, :])
         nc.sync.dma_start(w_codes[:].bitcast(I32), w1_words[0].bitcast(I32))
         nc.sync.dma_start(cache[:], mem)
         nc.sync.dma_start(slot_sb[:], slot)
 
         for j in EARLY_ROWS:
             for h in range(2):
-                picked = raw[j][:].indirect(entries(offs_sb, h * HALF, HALF))
+                picked = raw[j].indirect(entries(offs_sb, h * HALF, HALF))
                 target = grouped[:, h * HALF : (h + 1) * HALF, j]
-                if (j, h) == (EARLY_ROWS[0], 1):
-                    early = keep.tile([P, HALF], BF16, name="early")
+                if h == 1:
+                    early = keep.tile([P, HALF], F32, name=f"early{j}")
                     nc.scalar.activation(early[:], picked, COPY)
                     nc.vector.tensor_copy(target, early[:])
                 else:
@@ -73,7 +73,7 @@ def tile_picked_kvput_none_e_kernel(tc, xT, mem, w1_words, w1_scales, offs, slot
 
         def fetch(at, count, on_vector, tag):
             plain.setdefault(at, keep.tile([P, count], BF16, name=f"plain{at}", tag=tag))
-            picked = raw[LAST_ROW][:].indirect(entries(offs_sb, at, count))
+            picked = raw[LAST_ROW].indirect(entries(offs_sb, at, count))
             if on_vector:
                 nc.vector.tensor_copy(plain[at][:], picked)
             else:

@@ -50,9 +50,14 @@ def tile_picked_kvput_none_e_kernel(tc, xT, mem, w1_words, w1_scales, offs, slot
         nc.sync.dma_start(pair[:], x_rows[:, 0:2, :])
         nc.sync.dma_start(offs_sb[:], offs)
         nc.sync.dma_start(raw[2], x_rows[:, 2, :])
-        for q in range(4):
-            nc.sync.dma_start(w_scales[32 * q : 32 * q + 4, :].bitcast(I32), w1_scales[0, 4 * q : 4 * q + 4, :].bitcast(I32))
+        def scale_rows(first):
+            for q in range(4):
+                rows = w1_scales[0, 4 * q + first : 4 * q + first + 2, :]
+                nc.sync.dma_start(w_scales[32 * q + first : 32 * q + first + 2, :].bitcast(I32), rows.bitcast(I32))
+
+        scale_rows(0)
         nc.sync.dma_start(raw[LAST_ROW], x_rows[:, LAST_ROW, :])
+        scale_rows(2)
         nc.sync.dma_start(w_codes[:].bitcast(I32), w1_words[0].bitcast(I32))
         nc.sync.dma_start(cache[:], mem)
         nc.sync.dma_start(slot_sb[:], slot)

@@ -50,14 +50,14 @@ def tile_picked_kvput_none_e_kernel(tc, xT, mem, w1_words, w1_scales, offs, slot
         nc.sync.dma_start(pair[:], x_rows[:, 0:2, :])
         nc.sync.dma_start(offs_sb[:], offs)
         nc.sync.dma_start(raw[2], x_rows[:, 2, :])
-        def scale_rows(first):
-            for q in range(4):
-                rows = w1_scales[0, 4 * q + first : 4 * q + first + 2, :]
-                nc.sync.dma_start(w_scales[32 * q + first : 32 * q + first + 2, :].bitcast(I32), rows.bitcast(I32))
+        def scale_rows(halves):
+            for h in halves:
+                place = 32 * (h // 2) + 2 * (h % 2)
+                nc.sync.dma_start(w_scales[place : place + 2, :].bitcast(I32), w1_scales[0, 2 * h : 2 * h + 2, :].bitcast(I32))
 
-        scale_rows(0)
+        scale_rows(range(0, 3))
         nc.sync.dma_start(raw[LAST_ROW], x_rows[:, LAST_ROW, :])
-        scale_rows(2)
+        scale_rows(range(3, 8))
         nc.sync.dma_start(w_codes[:].bitcast(I32), w1_words[0].bitcast(I32))
         nc.sync.dma_start(cache[:], mem)
         nc.sync.dma_start(slot_sb[:], slot)

@@ -20,8 +20,7 @@ PACK = 4
 HALF = S // 2
 EARLY_ROWS = (0, 1, 2)
 LAST_ROW = 3
-PIECE = 256
-SCALAR_SCATTERS = (384,)
+PIECE = 128
 
 
 def entries(lst, first, count):
@@ -63,21 +62,15 @@ def tile_picked_kvput_none_e_kernel(tc, xT, mem, w1_words, w1_scales, offs, slot
         nc.sync.dma_start(slot_sb[:], slot)
 
         for j in EARLY_ROWS:
-            for h in range(2):
-                picked = raw[j].indirect(entries(offs_sb, h * HALF, HALF))
-                target = grouped[:, h * HALF : (h + 1) * HALF, j]
-                if h == 1:
-                    early = keep.tile([P, HALF], F32, name=f"early{j}")
-                    nc.scalar.activation(early[:], picked, COPY)
-                    nc.vector.tensor_copy(target, early[:])
-                else:
-                    nc.vector.tensor_copy(target, picked)
+            nc.vector.tensor_copy(grouped[:, :HALF, j], raw[j].indirect(entries(offs_sb, 0, HALF)))
+            early = keep.tile([P, HALF], F32, name=f"early{j}")
+            nc.scalar.activation(early[:], raw[j].indirect(entries(offs_sb, HALF, HALF)), COPY)
+            nc.vector.tensor_copy(grouped[:, HALF:, j], early[:])
 
-        short = PIECE // 2
         plain = dict()
 
         def fetch(at, count, on_vector, tag):
-            plain.setdefault(at, keep.tile([P, count], BF16, name=f"plain{at}", tag=tag))
+            plain.setdefault(at, keep.tile([P, count], BF16, name=f"plain{at}", tag=tag, align_bytes=64))
             picked = raw[LAST_ROW].indirect(entries(offs_sb, at, count))
             if on_vector:
                 nc.vector.tensor_copy(plain[at][:], picked)
@@ -87,49 +80,50 @@ def tile_picked_kvput_none_e_kernel(tc, xT, mem, w1_words, w1_scales, offs, slot
         def weave(at, count):
             nc.vector.tensor_copy(grouped[:, at : at + count, LAST_ROW], plain[at][:])
 
-        def project(first, widths, copy):
-            acc = psum.tile([N, sum(widths)], F32, name=f"acc{first}")
-            at = first
-            for width in widths:
-                codes = keep.tile([P, width], U32, name=f"codes{at}", align_bytes=64)
-                scales = keep.tile([P, width], U8, name=f"scales{at}", align_bytes=64)
-                nc.vector.quantize_mx(
-                    out=codes[:].bitcast(FP8X4),
-                    scales=scales[:],
-                    in_=grouped[:, at : at + width, :].rearrange("p n j -> p (n j)"),
-                )
-                nc.tensor.matmul_mx(
-                    out=acc[:, at - first : at - first + width],
-                    lhsT=w_codes[:].bitcast(FP4X4),
-                    lhsT_scale=w_scales[:],
-                    rhs=codes[:].bitcast(FP8X4),
-                    rhs_scale=scales[:],
-                    start=True,
-                    stop=True,
-                )
-                at = at + width
-            copy(y[:, first:at], acc[:])
+        def project(at, width, copy, tag=None):
+            acc = psum.tile([N, width], F32, name=f"acc{at}")
+            codes = keep.tile([P, width], U32, name=f"codes{at}", tag=tag or f"codes{at}", align_bytes=64)
+            scales = keep.tile([P, width], U8, name=f"scales{at}", align_bytes=64)
+            nc.vector.quantize_mx(
+                out=codes[:].bitcast(FP8X4),
+                scales=scales[:],
+                in_=grouped[:, at : at + width, :].rearrange("p n j -> p (n j)"),
+            )
+            nc.tensor.matmul_mx(
+                out=acc[:],
+                lhsT=w_codes[:].bitcast(FP4X4),
+                lhsT_scale=w_scales[:],
+                rhs=codes[:].bitcast(FP8X4),
+                rhs_scale=scales[:],
+                start=True,
+                stop=True,
+            )
+            if copy is not None:
+                copy(y[:, at : at + width], acc[:])
+            return acc
 
-        lead, last = 3 * short, S - 192
-        fetch(0, short, True, "a")
-        fetch(short, short, False, "b")
-        fetch(2 * short, short, False, "c")
-        fetch(lead, last - lead, False, "d")
-        for at in range(0, lead, short):
-            weave(at, short)
-        for at in range(0, lead, short):
-            project(at, (short,), nc.scalar.copy)
-        fetch(last, S - last, True, "c")
-        weave(lead, last - lead)
-        weave(last, S - last)
-        project(lead, (PIECE,), nc.vector.tensor_copy)
-        project(lead + PIECE, (PIECE,), nc.vector.tensor_copy)
-        project(lead + HALF, (short,), nc.vector.tensor_copy)
+        fetch(0, PIECE, True, "a")
+        fetch(PIECE, PIECE, False, "b")
+        fetch(2 * PIECE, PIECE, False, "c")
+        fetch(3 * PIECE, 2 * PIECE, False, "d")
+        fetch(5 * PIECE, 2 * PIECE, False, "f")
+        for i in range(3):
+            weave(i * PIECE, PIECE)
+        for i in range(2):
+            project(i * PIECE, PIECE, nc.scalar.copy)
+        third = project(2 * PIECE, PIECE, None)
+        share = 5 * PIECE // 2
+        nc.scalar.copy(y[:, 2 * PIECE : share], third[:, : share - 2 * PIECE])
+        nc.scalar.copy(y[:, share : 3 * PIECE], third[:, share - 2 * PIECE :])
+        weave(3 * PIECE, 2 * PIECE)
+        fetch(7 * PIECE, PIECE, True, "c")
+        project(3 * PIECE, 2 * PIECE, nc.vector.tensor_copy)
+        weave(5 * PIECE, 2 * PIECE)
+        weave(7 * PIECE, PIECE)
+        for i in (5, 6, 7):
+            project(i * PIECE, PIECE, nc.vector.tensor_copy)
 
-        at = 0
-        for count in SCALAR_SCATTERS:
-            nc.scalar.activation(cache[:].indirect(entries(slot_sb, at, count)), y[:, at : at + count], COPY)
-            at = at + count
-        nc.vector.tensor_copy(cache[:].indirect(entries(slot_sb, at, S - at)), y[:, at:])
+        nc.scalar.activation(cache[:].indirect(entries(slot_sb, 0, share)), y[:, :share], COPY)
+        nc.vector.tensor_copy(cache[:].indirect(entries(slot_sb, share, S - share)), y[:, share:])
 
         nc.sync.dma_start(out, cache[:])

@@ -21,6 +21,7 @@ HALF = S // 2
 EARLY_ROWS = (0, 1, 2)
 LAST_ROW = 3
 PIECE = 128
+LATE = 192
 
 
 def entries(lst, first, count):
@@ -106,7 +107,7 @@ def tile_picked_kvput_none_e_kernel(tc, xT, mem, w1_words, w1_scales, offs, slot
         fetch(PIECE, PIECE, False, "b")
         fetch(2 * PIECE, PIECE, False, "c")
         fetch(3 * PIECE, 2 * PIECE, False, "d")
-        fetch(5 * PIECE, 2 * PIECE, False, "f")
+        fetch(5 * PIECE, S - LATE - 5 * PIECE, False, "f")
         for i in range(3):
             weave(i * PIECE, PIECE)
         for i in range(2):
@@ -116,10 +117,10 @@ def tile_picked_kvput_none_e_kernel(tc, xT, mem, w1_words, w1_scales, offs, slot
         nc.scalar.copy(y[:, 2 * PIECE : share], third[:, : share - 2 * PIECE])
         nc.scalar.copy(y[:, share : 3 * PIECE], third[:, share - 2 * PIECE :])
         weave(3 * PIECE, 2 * PIECE)
-        fetch(7 * PIECE, PIECE, True, "c")
+        fetch(S - LATE, LATE, True, "c")
         project(3 * PIECE, 2 * PIECE, nc.vector.tensor_copy)
-        weave(5 * PIECE, 2 * PIECE)
-        weave(7 * PIECE, PIECE)
+        weave(5 * PIECE, S - LATE - 5 * PIECE)
+        weave(S - LATE, LATE)
         for i in (5, 6, 7):
             project(i * PIECE, PIECE, nc.vector.tensor_copy)
 

@@ -21,6 +21,7 @@ HALF = S // 2
 EARLY_ROWS = (0, 1, 2)
 LAST_ROW = 3
 PIECE = 128
+BURST = 256
 LATE = 192
 
 
@@ -38,10 +39,10 @@ def tile_picked_kvput_none_e_kernel(tc, xT, mem, w1_words, w1_scales, offs, slot
 
         offs_sb = keep.tile([P, S // 16], U16, name="offs_sb")
         slot_sb = keep.tile([P, S // 16], U16, name="slot_sb")
-        pair = keep.tile([P, 2, T], F32, name="pair")
-        raw = [pair[:, 0, :], pair[:, 1, :]] + [keep.tile([P, T], F32, name=f"raw{j}")[:] for j in (2, 3)]
-        cache = keep.tile([P, U], F32, name="cache")
-        w_codes = keep.tile([P, 2 * N], U8, name="w_codes", align_bytes=64)
+        pair = keep.tile([P, 2, T], F32, name="pair", align_bytes=BURST)
+        raw = [pair[:, 0, :], pair[:, 1, :]] + [keep.tile([P, T], F32, name=f"raw{j}", align_bytes=BURST)[:] for j in (2, 3)]
+        cache = keep.tile([P, U], F32, name="cache", align_bytes=BURST)
+        w_codes = keep.tile([P, 2 * N], U8, name="w_codes", align_bytes=BURST)
         w_scales = keep.tile([P, N], U8, name="w_scales", align_bytes=64)
         grouped = keep.tile([P, S, PACK], BF16, name="grouped", align_bytes=64)
         y = keep.tile([P, S], F32, name="y")

@@ -37,15 +37,15 @@ def tile_picked_kvput_none_e_kernel(tc, xT, mem, w1_words, w1_scales, offs, slot
         keep = ctx.enter_context(tc.tile_pool(name="keep", bufs=1))
         psum = ctx.enter_context(tc.psum_pool(name="psum", bufs=1))
 
-        offs_sb = keep.tile([P, S // 16], U16, name="offs_sb")
-        slot_sb = keep.tile([P, S // 16], U16, name="slot_sb")
+        offs_sb = keep.tile([P, S // 16], U16, name="offs_sb", align_bytes=BURST)
+        slot_sb = keep.tile([P, S // 16], U16, name="slot_sb", align_bytes=BURST)
         pair = keep.tile([P, 2, T], F32, name="pair", align_bytes=BURST)
         raw = [pair[:, 0, :], pair[:, 1, :]] + [keep.tile([P, T], F32, name=f"raw{j}", align_bytes=BURST)[:] for j in (2, 3)]
         cache = keep.tile([P, U], F32, name="cache", align_bytes=BURST)
         w_codes = keep.tile([P, 2 * N], U8, name="w_codes", align_bytes=BURST)
-        w_scales = keep.tile([P, N], U8, name="w_scales", align_bytes=64)
-        grouped = keep.tile([P, S, PACK], BF16, name="grouped", align_bytes=64)
-        y = keep.tile([P, S], F32, name="y")
+        w_scales = keep.tile([P, N], U8, name="w_scales", align_bytes=BURST)
+        grouped = keep.tile([P, S, PACK], BF16, name="grouped", align_bytes=BURST)
+        y = keep.tile([P, S], F32, name="y", align_bytes=BURST)
 
         nc.vector.memset(w_scales[:].bitcast(I32), 0)
         nc.sync.dma_start(pair[:], x_rows[:, 0:2, :])
@@ -65,14 +65,14 @@ def tile_picked_kvput_none_e_kernel(tc, xT, mem, w1_words, w1_scales, offs, slot
 
         for j in EARLY_ROWS:
             nc.vector.tensor_copy(grouped[:, :HALF, j], raw[j].indirect(entries(offs_sb, 0, HALF)))
-            early = keep.tile([P, HALF], F32, name=f"early{j}")
+            early = keep.tile([P, HALF], F32, name=f"early{j}", align_bytes=BURST)
             nc.scalar.activation(early[:], raw[j].indirect(entries(offs_sb, HALF, HALF)), COPY)
             nc.vector.tensor_copy(grouped[:, HALF:, j], early[:])
 
         plain = dict()
 
         def fetch(at, count, on_vector, tag):
-            plain.setdefault(at, keep.tile([P, count], BF16, name=f"plain{at}", tag=tag, align_bytes=64))
+            plain.setdefault(at, keep.tile([P, count], BF16, name=f"plain{at}", tag=tag, align_bytes=BURST))
             picked = raw[LAST_ROW].indirect(entries(offs_sb, at, count))
             if on_vector:
                 nc.vector.tensor_copy(plain[at][:], picked)
@@ -84,8 +84,8 @@ def tile_picked_kvput_none_e_kernel(tc, xT, mem, w1_words, w1_scales, offs, slot
 
         def project(at, width, copy, tag=None):
             acc = psum.tile([N, width], F32, name=f"acc{at}")
-            codes = keep.tile([P, width], U32, name=f"codes{at}", tag=tag or f"codes{at}", align_bytes=64)
-            scales = keep.tile([P, width], U8, name=f"scales{at}", align_bytes=64)
+            codes = keep.tile([P, width], U32, name=f"codes{at}", tag=tag or f"codes{at}", align_bytes=BURST)
+            scales = keep.tile([P, width], U8, name=f"scales{at}", align_bytes=BURST)
             nc.vector.quantize_mx(
                 out=codes[:].bitcast(FP8X4),
                 scales=scales[:],

from contextlib import ExitStack

import concourse.mybir as mybir

K, T, S, N, U = 512, 4096, 1024, 128, 2048
FLOPS = 2 * K * N * S

F32 = mybir.dt.float32
BF16 = mybir.dt.bfloat16
I32 = mybir.dt.int32
U32 = mybir.dt.uint32
U16 = mybir.dt.uint16
U8 = mybir.dt.uint8
FP8X4 = mybir.dt.float8_e4m3fn_x4
FP4X4 = mybir.dt.float4_e2m1fn_x4
COPY = mybir.ActivationFunctionType.Copy

P = 128
PACK = 4
HALF = S // 2
EARLY_ROWS = (0, 1, 2)
LAST_ROW = 3
PIECE = 128
BURST = 256
LATE = 192


def entries(lst, first, count):
    return lst[:, first // 16 : (first + count) // 16]


def tile_picked_kvput_none_e_kernel(tc, xT, mem, w1_words, w1_scales, offs, slot, out):
    nc = tc.nc
    x_rows = xT.rearrange("(p j) t -> p j t", j=PACK)

    with ExitStack() as ctx:
        keep = ctx.enter_context(tc.tile_pool(name="keep", bufs=1))
        psum = ctx.enter_context(tc.psum_pool(name="psum", bufs=1))

        offs_sb = keep.tile([P, S // 16], U16, name="offs_sb", align_bytes=BURST)
        slot_sb = keep.tile([P, S // 16], U16, name="slot_sb", align_bytes=BURST)
        pair = keep.tile([P, 2, T], F32, name="pair", align_bytes=BURST)
        raw = [pair[:, 0, :], pair[:, 1, :]] + [keep.tile([P, T], F32, name=f"raw{j}", align_bytes=BURST)[:] for j in (2, 3)]
        cache = keep.tile([P, U], F32, name="cache", align_bytes=BURST)
        w_codes = keep.tile([P, 2 * N], U8, name="w_codes", align_bytes=BURST)
        w_scales = keep.tile([P, N], U8, name="w_scales", align_bytes=BURST)
        grouped = keep.tile([P, S, PACK], BF16, name="grouped", align_bytes=BURST)
        y = keep.tile([P, S], F32, name="y", align_bytes=BURST)

        nc.vector.memset(w_scales[:].bitcast(I32), 0)
        nc.sync.dma_start(pair[:], x_rows[:, 0:2, :])
        nc.sync.dma_start(offs_sb[:], offs)
        nc.sync.dma_start(raw[2], x_rows[:, 2, :])
        def scale_rows(halves):
            for h in halves:
                place = 32 * (h // 2) + 2 * (h % 2)
                nc.sync.dma_start(w_scales[place : place + 2, :].bitcast(I32), w1_scales[0, 2 * h : 2 * h + 2, :].bitcast(I32))

        scale_rows(range(0, 3))
        nc.sync.dma_start(raw[LAST_ROW], x_rows[:, LAST_ROW, :])
        scale_rows(range(3, 8))
        nc.sync.dma_start(w_codes[:].bitcast(I32), w1_words[0].bitcast(I32))
        nc.sync.dma_start(cache[:], mem)
        nc.sync.dma_start(slot_sb[:], slot)

        for j in EARLY_ROWS:
            nc.vector.tensor_copy(grouped[:, :HALF, j], raw[j].indirect(entries(offs_sb, 0, HALF)))
            early = keep.tile([P, HALF], F32, name=f"early{j}", align_bytes=BURST)
            nc.scalar.activation(early[:], raw[j].indirect(entries(offs_sb, HALF, HALF)), COPY)
            nc.vector.tensor_copy(grouped[:, HALF:, j], early[:])

        plain = dict()

        def fetch(at, count, on_vector, tag):
            plain.setdefault(at, keep.tile([P, count], BF16, name=f"plain{at}", tag=tag, align_bytes=BURST))
            picked = raw[LAST_ROW].indirect(entries(offs_sb, at, count))
            if on_vector:
                nc.vector.tensor_copy(plain[at][:], picked)
            else:
                nc.scalar.activation(plain[at][:], picked, COPY)

        def weave(at, count):
            nc.vector.tensor_copy(grouped[:, at : at + count, LAST_ROW], plain[at][:])

        def project(at, width, copy, tag=None):
            acc = psum.tile([N, width], F32, name=f"acc{at}")
            codes = keep.tile([P, width], U32, name=f"codes{at}", tag=tag or f"codes{at}", align_bytes=BURST)
            scales = keep.tile([P, width], U8, name=f"scales{at}", align_bytes=BURST)
            nc.vector.quantize_mx(
                out=codes[:].bitcast(FP8X4),
                scales=scales[:],
                in_=grouped[:, at : at + width, :].rearrange("p n j -> p (n j)"),
            )
            nc.tensor.matmul_mx(
                out=acc[:],
                lhsT=w_codes[:].bitcast(FP4X4),
                lhsT_scale=w_scales[:],
                rhs=codes[:].bitcast(FP8X4),
                rhs_scale=scales[:],
                start=True,
                stop=True,
            )
            if copy is not None:
                copy(y[:, at : at + width], acc[:])
            return acc

        fetch(0, PIECE, True, "a")
        fetch(PIECE, PIECE, False, "b")
        fetch(2 * PIECE, PIECE, False, "c")
        fetch(3 * PIECE, 2 * PIECE, False, "d")
        fetch(5 * PIECE, S - LATE - 5 * PIECE, False, "f")
        for i in range(3):
            weave(i * PIECE, PIECE)
        for i in range(2):
            project(i * PIECE, PIECE, nc.scalar.copy)
        third = project(2 * PIECE, PIECE, None)
        share = 5 * PIECE // 2
        nc.scalar.copy(y[:, 2 * PIECE : share], third[:, : share - 2 * PIECE])
        nc.scalar.copy(y[:, share : 3 * PIECE], third[:, share - 2 * PIECE :])
        weave(3 * PIECE, 2 * PIECE)
        fetch(S - LATE, LATE, True, "c")
        project(3 * PIECE, 2 * PIECE, nc.vector.tensor_copy)
        weave(5 * PIECE, S - LATE - 5 * PIECE)
        weave(S - LATE, LATE)
        for i in (5, 6, 7):
            project(i * PIECE, PIECE, nc.vector.tensor_copy)

        nc.scalar.activation(cache[:].indirect(entries(slot_sb, 0, share)), y[:, :share], COPY)
        nc.vector.tensor_copy(cache[:].indirect(entries(slot_sb, share, S - share)), y[:, share:])

        nc.sync.dma_start(out, cache[:])
